import numpy as np
import ml_dtypes


def mxq(x, axis, fmt="e4m3"):
    dtype, down = {"e4m3": (ml_dtypes.float8_e4m3fn, 7), "e5m2": (ml_dtypes.float8_e5m2, 14)}[fmt]
    v = np.moveaxis(np.asarray(x, np.float32).astype(ml_dtypes.bfloat16).astype(np.float64), axis, -1)
    blocks = v.reshape(v.shape[:-1] + (-1, 32))
    amax = np.abs(blocks).max(-1, keepdims=True)
    byte = np.maximum(np.where(amax > 0, np.frexp(amax)[1] - 1 + 127, 0) - down, 1)
    scale = np.exp2(byte - 127.0)
    codes = (blocks / scale).astype(np.float32).astype(dtype).astype(np.float64)
    return np.moveaxis((codes * scale).reshape(v.shape), -1, axis)


WIDE = False


def mx_kscale(k):
    if not WIDE:
        return np.ones(k)
    levels = np.array([10, -10, 5, -5, 0])
    if k % 512:
        return np.exp2(np.random.permutation(np.resize(levels, k // 32))).repeat(32)
    a = np.empty((k // 512, 16))
    for p in range(k // 512):
        a[p, :8] = np.random.permutation(np.resize(levels, 8))
        for g in range(8):
            far = levels[np.abs(levels - a[p, g]) >= 10]
            a[p, g + 8] = far[np.random.randint(len(far))]
    return np.exp2(a.ravel()).repeat(32)


def f64(x):
    return np.asarray(x).astype(np.float64)


def striped(idx):
    return np.tile(idx.reshape(-1, 16).T, (8, 1)).astype(np.uint16)


def unstriped(offs):
    return offs[:16].T.reshape(-1).astype(np.int64)


E2M1 = np.array([0.0, 0.5, 1.0, 1.5, 2.0, 3.0, 4.0, 6.0, -0.0, -0.5, -1.0, -1.5, -2.0, -3.0, -4.0, -6.0])


def pack_weight(w, fmt):
    k, n = w.shape
    w = f64(np.asarray(w, np.float32).astype(ml_dtypes.bfloat16)).reshape(k // 32, 32, n)
    amax = np.abs(w).max(1)
    if fmt == "e4m3":
        byte = np.frexp(amax)[1] - 1 + 127 - 7
    else:
        mant, ex = np.frexp(amax / 6.0)
        byte = np.where(mant > 0.5, ex, ex - 1) + 127
    byte = np.clip(np.where(amax > 0, byte, 1), 1, 254)
    scaled = (w * np.exp2(127.0 - byte)[:, None, :]).reshape(k, n).astype(np.float32)
    by_word = np.ascontiguousarray(scaled.reshape(k // 512, 128, 4, n).transpose(0, 1, 3, 2))
    if fmt == "e4m3":
        words = by_word.astype(ml_dtypes.float8_e4m3fn).view(np.uint8)
    else:
        c = by_word.astype(ml_dtypes.float4_e2m1fn).view(np.uint8) & 0xF
        words = (c[..., 0::2] | (c[..., 1::2] << 4)).reshape(k // 512, 128, 2 * n)
    return np.ascontiguousarray(words), np.ascontiguousarray(byte.astype(np.uint8).reshape(k // 512, 16, n))


def unpack_weight(words, scales, fmt):
    g, _, n = scales.shape
    words = np.ascontiguousarray(words).reshape(g, 128, n, -1)
    if fmt == "e4m3":
        vals = words.view(ml_dtypes.float8_e4m3fn).astype(np.float64)
    else:
        nib = np.empty((g, 128, n, 4), np.uint8)
        nib[..., 0::2] = words & 0xF
        nib[..., 1::2] = words >> 4
        vals = E2M1[nib]
    vals = vals * np.repeat(np.exp2(scales.astype(np.float64) - 127.0), 8, axis=1)[..., None]
    return vals.transpose(0, 1, 3, 2).reshape(g * 512, n)


def gelu(v):
    return 0.5 * v * (1.0 + np.tanh(np.sqrt(2.0 / np.pi) * (v + 0.044715 * v**3)))


K, T, S, M, H, N, T2, P = 1024, 2048, 1024, 512, 1024, 512, 2048, 1024


def setup_inputs():
    n = np.random.standard_normal
    s = mx_kscale(K)[:, None]
    c = mx_kscale(M)[:, None]
    u = mx_kscale(H)[:, None]
    d = {}
    d["tab_words"], d["tab_scales"] = pack_weight(n((K, T)) * s, "e4m3")
    d["offs"] = striped(np.random.permutation(T)[:S])
    d["w1"] = (1.5 * n((K, M)) / s / K**0.5).astype(np.float32)
    d["gain1"] = (np.exp(0.3 * n(M)) * c[:, 0]).astype(np.float32)
    d["w2_words"], d["w2_scales"] = pack_weight(1.5 * n((M, H)) / c * u.T / M**0.5, "e2m1")
    d["rest"] = (0.8 * n((H, S)) * u).astype(np.float32)
    d["wgs"] = np.exp(0.3 * n((128, S))).astype(np.float32)
    d["page0"] = (1.2 * n((H, T2)) * u).astype(np.float32)
    d["offs2"] = striped(np.random.permutation(T2)[:S])
    d["offs3"] = striped(np.random.permutation(T2)[:P])
    d["gain2"] = np.exp(0.4 * n(H)).astype(np.float32)
    d["w3"] = (1.2 * n((H, N)) / u / H**0.5).astype(np.float32)
    d["wgo"] = np.exp(0.3 * n((128, P))).astype(np.float32)
    d["page1"] = (0.5 * n((N, T2))).astype(np.float32)
    d["offs4"] = striped(np.random.permutation(T2)[:P])
    return d


def reference(tab_words, tab_scales, offs, w1, gain1, w2_words, w2_scales, rest, wgs, page0, offs2, offs3, gain2, w3, wgo, page1, offs4):
    v = unpack_weight(tab_words, tab_scales, "e4m3")[:, unstriped(offs)]
    f = np.tanh(mxq(f64(w1), 0, "e4m3").T @ v) * f64(gain1)[:, None]
    w2 = unpack_weight(w2_words, w2_scales, "e2m1")
    h = (w2.T @ mxq(f, 0, "e4m3")) - f64(rest)
    page = f64(page0).copy()
    page[:, unstriped(offs2)] = np.tile(f64(wgs), (H // 128, 1)) * h
    x = page[:, unstriped(offs3)] * f64(gain2)[:, None]
    e = mxq(f64(w3), 0, "e4m3").T @ mxq(x, 0, "e4m3")
    y = e / (1.0 + np.abs(e))
    out = f64(page1).copy()
    out[:, unstriped(offs4)] = np.tile(f64(wgo), (N // 128, 1)) * y
    return out

@@ -1,0 +1,381 @@
+from contextlib import ExitStack
+
+import concourse.mybir as mybir
+from concourse.masks import make_identity
+
+K, T, S, M, H, N, T2, PK = 1024, 2048, 1024, 512, 1024, 512, 2048, 1024
+FLOPS = 2 * K * M * S + 2 * M * H * S + 2 * H * N * PK
+
+F32 = mybir.dt.float32
+BF16 = mybir.dt.bfloat16
+I32 = mybir.dt.int32
+U32 = mybir.dt.uint32
+U16 = mybir.dt.uint16
+U8 = mybir.dt.uint8
+FP8X4 = mybir.dt.float8_e4m3fn_x4
+FP4X4 = mybir.dt.float4_e2m1fn_x4
+ACT = mybir.ActivationFunctionType
+ALU = mybir.AluOpType
+
+P = 128
+QUARTER = 256
+HALF = 512
+SLICES = 8
+REST_RING = 5
+NEG_RING = 2
+TURN_RING = 3
+
+
+def tile_list_socket_liner_page_kernel(
+    tc, tab_words, tab_scales, offs, w1, gain1, w2_words, w2_scales, rest, wgs,
+    page0, offs2, offs3, gain2, w3, wgo, page1, offs4, out,
+):
+    nc = tc.nc
+    with ExitStack() as ctx:
+        lists = ctx.enter_context(tc.tile_pool(name="lists", bufs=1))
+        pool = ctx.enter_context(tc.tile_pool(name="pool", bufs=1))
+        psum = ctx.enter_context(tc.psum_pool(name="psum", bufs=1))
+
+        def sb(name, shape, dtype, tag=None):
+            return pool.tile(shape, dtype, name=name, tag=tag or name, align_bytes=64)
+
+        def cols(lst, lo, hi):
+            return lst[:, lo // 16 : hi // 16]
+
+        banks = [psum.tile([P, HALF], F32, name="bank%d" % b) for b in range(8)]
+
+        scan_list = lists.tile([P, S // 16], U16, name="scan_list")
+        put_list = lists.tile([P, S // 16], U16, name="put_list")
+        recall_list = lists.tile([P, PK // 16], U16, name="recall_list")
+        out_list = lists.tile([P, PK // 16], U16, name="out_list")
+
+        tab_plane = sb("tab_plane", [P, T], U8)
+        w2_plane = sb("w2_plane", [P, H], U8)
+        nc.vector.memset(tab_plane[:].bitcast(I32), 0)
+        nc.vector.memset(w2_plane[:].bitcast(I32), 0)
+
+        nc.sync.dma_start(scan_list[:], offs)
+        w2_raw = sb("w2_raw", [P, 2 * H], U8)
+        nc.sync.dma_start(w2_raw[:].bitcast(I32), w2_words[0].bitcast(I32))
+        for q in range(4):
+            nc.scalar.dma_start(
+                tab_plane[32 * q : 32 * q + 8, :].bitcast(I32),
+                tab_scales[:, 4 * q : 4 * q + 4, :].bitcast(I32),
+            )
+        for q in range(4):
+            nc.scalar.dma_start(
+                w2_plane[32 * q : 32 * q + 4, :].bitcast(I32),
+                w2_scales[0, 4 * q : 4 * q + 4, :].bitcast(I32),
+            )
+        w1_raw = [sb("w1_raw%d" % a, [P, 4, M], F32, tag="w_raw%d" % a) for a in range(2)]
+        for a in range(2):
+            nc.sync.dma_start(
+                w1_raw[a][:], w1[HALF * a : HALF * (a + 1), :].rearrange("(p j) m -> p j m", j=4)
+            )
+        tab = [sb("tab%d" % a, [P, T], I32, tag="tab%d" % a) for a in range(2)]
+        for a in range(2):
+            nc.sync.dma_start(tab[a][:], tab_words[a].rearrange("p t i -> p (t i)").bitcast(I32))
+        g1 = sb("g1", [P, 4], F32)
+        nc.sync.dma_start(g1[:], gain1.rearrange("(p t) -> p t", t=4))
+
+        rest_rows = rest.rearrange("(a p t) j -> a t p j", a=2, t=4)
+        page_rows = page0.rearrange("(a p t) c -> a t p c", a=2, t=4)
+        wgs_rows = wgs.rearrange("(q t) j -> q t j", t=4)
+        ring = [sb("ring%d" % i, [P, S], F32) for i in range(REST_RING)]
+        pages = [sb("page%d" % s, [P, T2], F32) for s in range(SLICES)]
+        wg_first = sb("wg_first", [P, S], F32)
+        wg_rest = sb("wg_rest", [P, 3, S], F32)
+        g2 = sb("g2", [P, 2, 4], F32)
+
+        def rest_tile(s):
+            return ring[s % REST_RING]
+
+        def wg(s):
+            t = s % 4
+            return wg_first[:] if t == 0 else wg_rest[:, t - 1, :]
+
+        def load_slice(s):
+            nc.sync.dma_start(rest_tile(s)[:], rest_rows[s // 4, s % 4])
+            if s == 0:
+                nc.sync.dma_start(put_list[:], offs2)
+                for u in range(4):
+                    nc.sync.dma_start(wg_first[32 * u : 32 * u + 32, :], wgs_rows[:, 0, :])
+            nc.sync.dma_start(pages[s][:], page_rows[s // 4, s % 4])
+            if s == 0:
+                nc.sync.dma_start(rest_tile(1)[:], rest_rows[0, 1])
+                for u in range(4):
+                    nc.sync.dma_start(wg_rest[32 * u : 32 * u + 32, :, :], wgs_rows[:, 1:4, :])
+
+        load_slice(0)
+        nc.sync.dma_start(pages[1][:], page_rows[0, 1])
+        nc.sync.dma_start(recall_list[:], offs3)
+        nc.sync.dma_start(g2[:], gain2.rearrange("(a p t) -> p a t", a=2, t=4))
+        for s in range(2, REST_RING):
+            load_slice(s)
+
+        ident = sb("ident", [P, P], F32)
+        make_identity(nc, ident[:])
+
+        w2_dealt = sb("w2_dealt", [P, SLICES, 2 * P], U8)
+        w2_sc = sb("w2_sc", [P, SLICES, P], U8)
+        for a in range(2):
+            nc.vector.tensor_copy(
+                w2_dealt[:, 4 * a : 4 * a + 4, :].rearrange("p t (q b) -> p t q b", b=2),
+                w2_raw[:, H * a : H * (a + 1)].rearrange("p (q t b) -> p t q b", t=4, b=2),
+            )
+        nc.vector.tensor_copy(
+            w2_sc[:].rearrange("p (a t) q -> p a t q", a=2),
+            w2_plane[:].rearrange("p (a q t) -> p a t q", a=2, t=4),
+        )
+        v_sc = sb("v_sc", [P, S], U8)
+        nc.vector.tensor_copy(v_sc[:], tab_plane[:].indirect(scan_list[:]))
+
+        w1_bf = [sb("w1_bf%d" % a, [P, 4 * M], BF16, tag="w_bf%d" % a) for a in range(2)]
+        w1_codes = [sb("w1_codes%d" % a, [P, M], U32, tag="w_codes%d" % a) for a in range(2)]
+        w1_sc = [sb("w1_sc%d" % a, [P, M], U8, tag="w_sc%d" % a) for a in range(2)]
+        for a in range(2):
+            dst = w1_bf[a][:].rearrange("p (t m j) -> p m t j", t=4, j=4)
+            src = w1_raw[a][:].rearrange("p j (m t) -> p m t j", t=4)
+            if a == 0:
+                nc.scalar.copy(dst, src)
+            else:
+                nc.vector.tensor_copy(dst, src)
+        for a in range(2):
+            nc.vector.quantize_mx(w1_codes[a][:].bitcast(FP8X4), w1_sc[a][:], w1_bf[a][:])
+
+        v_codes = [sb("v_codes%d" % a, [P, S], U32, tag="codes%d" % a) for a in range(2)]
+        for lo in range(0, S, HALF):
+            nc.vector.tensor_copy(
+                v_codes[0][:, lo : lo + HALF], tab[0][:].bitcast(U32).indirect(cols(scan_list, lo, lo + HALF))
+            )
+        for lo in range(0, S, QUARTER):
+            nc.vector.tensor_copy(
+                v_codes[1][:, lo : lo + QUARTER],
+                tab[1][:].bitcast(U32).indirect(cols(scan_list, lo, lo + QUARTER)),
+            )
+
+        th = sb("th", [P, 2, 4 * QUARTER], F32, tag="wide")
+        f_planes = [sb("f_planes%d" % i, [P, 4, QUARTER], BF16) for i in range(2)]
+        f_bf = [sb("f_bf%d" % i, [P, 4 * QUARTER], BF16) for i in range(2)]
+        f_codes = sb("f_codes", [P, S], U32)
+        f_sc = sb("f_sc", [P, S], U8)
+
+        def second_product(s, lo, hi, bank):
+            nc.tensor.matmul_mx(
+                bank[:, 0 : hi - lo],
+                lhsT=w2_dealt[:, s, :].bitcast(FP4X4), lhsT_scale=w2_sc[:, s, :],
+                rhs=f_codes[:, lo:hi].bitcast(FP8X4), rhs_scale=f_sc[:, lo:hi],
+                start=True, stop=True,
+            )
+
+        def put(s, lo, hi):
+            nc.vector.tensor_tensor(
+                pages[s][:].indirect(cols(put_list, lo, hi)),
+                rest_tile(s)[:, lo:hi], wg(s)[:, lo:hi], ALU.mult,
+            )
+
+        def features(q):
+            lo, hi, i = QUARTER * q, QUARTER * (q + 1), q % 2
+            for t in range(4):
+                bank = banks[2 * i + t // 2]
+                for a in range(2):
+                    nc.tensor.matmul_mx(
+                        bank[:, QUARTER * (t % 2) : QUARTER * (t % 2 + 1)],
+                        lhsT=w1_codes[a][:, P * t : P * (t + 1)].bitcast(FP8X4),
+                        lhsT_scale=w1_sc[a][:, P * t : P * (t + 1)],
+                        rhs=v_codes[a][:, lo:hi].bitcast(FP8X4),
+                        rhs_scale=v_sc[4 * a : P, lo:hi],
+                        start=(a == 0), stop=(a == 1),
+                    )
+            for u in range(2):
+                nc.scalar.activation(th[:, i, HALF * u : HALF * (u + 1)], banks[2 * i + u][:], ACT.Tanh)
+                for t in (2 * u, 2 * u + 1):
+                    nc.scalar.activation(
+                        f_planes[i][:, t, :], th[:, i, QUARTER * t : QUARTER * (t + 1)],
+                        ACT.Copy, scale=g1[:, t : t + 1],
+                    )
+            nc.vector.tensor_copy(
+                f_bf[i][:].rearrange("p (c k t) -> p c t k", k=4, t=4),
+                f_planes[i][:].rearrange("p t (c k) -> p c t k", k=4),
+            )
+            nc.vector.quantize_mx(f_codes[:, lo:hi].bitcast(FP8X4), f_sc[:, lo:hi], f_bf[i][:])
+
+        def first_slice(q):
+            lo, hi = QUARTER * q, QUARTER * (q + 1)
+            bank = banks[4 + q % 2]
+            second_product(0, lo, hi, bank)
+            nc.vector.tensor_tensor(
+                rest_tile(0)[:, lo:hi], bank[:, 0:QUARTER], rest_tile(0)[:, lo:hi], ALU.subtract
+            )
+            put(0, lo, hi)
+
+        features(0)
+        for q in range(4):
+            if q + 1 < 4:
+                features(q + 1)
+            first_slice(q)
+
+        neg = [sb("neg%d" % i, [P, S], F32) for i in range(NEG_RING)]
+        turned = [sb("turned%d" % i, [P, S], F32) for i in range(TURN_RING)]
+
+        def states(s):
+            a_t, b_t, r_t = neg[s % NEG_RING], turned[s % TURN_RING], rest_tile(s)
+            for h in range(2):
+                lo = HALF * h
+                second_product(s, lo, lo + HALF, banks[4 + h])
+                nc.scalar.activation(a_t[:, lo : lo + HALF], banks[4 + h][:], ACT.Copy, scale=-1.0)
+            for h in range(2):
+                lo = HALF * h
+                for n, src in enumerate((r_t, a_t)):
+                    for c in range(4):
+                        nc.tensor.matmul(
+                            banks[6 + h][:, P * c : P * (c + 1)],
+                            lhsT=src[:, lo + P * c : lo + P * (c + 1)], rhs=ident[:],
+                            is_transpose=True, start=(n == 0 and c == 0), stop=(n == 1 and c == 3),
+                        )
+                nc.scalar.activation(b_t[:, lo : lo + HALF], banks[6 + h][:], ACT.Copy, scale=-1.0)
+            for h in range(2):
+                lo = HALF * h
+                for c in range(4):
+                    nc.tensor.transpose(
+                        banks[h][:, P * c : P * (c + 1)], b_t[:, lo + P * c : lo + P * (c + 1)], ident[:]
+                    )
+                nc.scalar.copy(r_t[:, lo : lo + HALF], banks[h][:])
+
+        def recall(s, lo, hi, dst):
+            nc.vector.tensor_copy(dst, pages[s][:].indirect(cols(recall_list, lo, hi)))
+
+        def weigh(s, src, dst):
+            a, t = s // 4, s % 4
+            nc.scalar.activation(
+                dst.rearrange("p (c t) -> p c t", t=4)[:, :, t], src, ACT.Copy, scale=g2[:, a, t : t + 1]
+            )
+
+        x_codes = [sb("x_codes%d" % a, [P, PK], U32, tag="codes%d" % a) for a in range(2)]
+        x_sc = [sb("x_sc%d" % a, [P, PK], U8) for a in range(2)]
+        w3_codes = [sb("w3_codes%d" % a, [P, N], U32, tag="w_codes%d" % a) for a in range(2)]
+        w3_sc = [sb("w3_sc%d" % a, [P, N], U8, tag="w_sc%d" % a) for a in range(2)]
+        w3_raw = [sb("w3_raw%d" % a, [P, 4, N], F32, tag="w_raw%d" % a) for a in range(2)]
+        w3_bf = [sb("w3_bf%d" % a, [P, 4 * N], BF16, tag="w_bf%d" % a) for a in range(2)]
+
+        def load_w3(a):
+            nc.sync.dma_start(
+                w3_raw[a][:], w3[HALF * a : HALF * (a + 1), :].rearrange("(p j) n -> p j n", j=4)
+            )
+
+        def quantize_w3(a):
+            nc.scalar.copy(
+                w3_bf[a][:].rearrange("p (c k j) -> p c j k", k=4, j=4),
+                w3_raw[a][:].rearrange("p j (c k) -> p c j k", k=4),
+            )
+            nc.vector.quantize_mx(w3_codes[a][:].bitcast(FP8X4), w3_sc[a][:], w3_bf[a][:])
+
+        x_bf0 = sb("x_bf0", [P, 4 * PK], BF16, tag="wide")
+        x_bf1a = sb("x_bf1a", [P, 4 * HALF], BF16, tag="x1a")
+
+        states(1)
+        put(1, 0, HALF)
+        put(1, HALF, S)
+        states(2)
+        for s in range(6):
+            got = turned[(s + 2) % TURN_RING]
+            wide = PK if s < 4 else HALF
+            recall(s, 0, wide, got[:, 0:wide])
+            put(s + 2, 0, S)
+            if s + REST_RING < SLICES:
+                load_slice(s + REST_RING)
+            if s in (0, 1):
+                load_w3(s)
+            if s + 3 < SLICES:
+                states(s + 3)
+            weigh(s, got[:, 0:wide], x_bf0[:] if s < 4 else x_bf1a[:])
+            if s in (1, 2):
+                quantize_w3(s - 1)
+            if s == 3:
+                nc.vector.quantize_mx(x_codes[0][:].bitcast(FP8X4), x_sc[0][:], x_bf0[:])
+
+        wo = sb("wo", [P, PK], F32)
+        nc.sync.dma_start(wo[:], wgo)
+        nc.sync.dma_start(out_list[:], offs4)
+        liner_tags = ("tab0", "tab1", "w_raw0", "w_raw1")
+        liners = [sb("liner%d" % n, [P, T2], F32, tag=liner_tags[n]) for n in range(4)]
+        for n in range(4):
+            nc.sync.dma_start(liners[n][:], page1[P * n : P * (n + 1), :])
+
+        got6, got7 = rest_tile(7), neg[7 % NEG_RING]
+        for lo in (0, HALF):
+            recall(6, lo, lo + HALF, got6[:, lo : lo + HALF])
+            recall(7, lo, lo + HALF, got7[:, lo : lo + HALF])
+        weigh(6, got6[:, 0:HALF], x_bf1a[:])
+        weigh(7, got7[:, 0:HALF], x_bf1a[:])
+        nc.vector.quantize_mx(x_codes[1][:, 0:HALF].bitcast(FP8X4), x_sc[1][:, 0:HALF], x_bf1a[:])
+        got45 = sb("got45", [P, 2, HALF], F32, tag="x1a")
+        for i in range(2):
+            recall(4 + i, HALF, PK, got45[:, i, :])
+
+        e_banks = ((0, 1, 6, 7), (2, 3, 4, 5))
+        inv_tiles = [ring[i] for i in (3, 4, 0, 1)]
+
+        def inv(h, n):
+            return inv_tiles[2 * h + n // 2][:, HALF * (n % 2) : HALF * (n % 2 + 1)]
+
+        def third_product(h, n):
+            lo = HALF * h
+            for a in range(2):
+                nc.tensor.matmul_mx(
+                    banks[e_banks[h][n]][:],
+                    lhsT=w3_codes[a][:, P * n : P * (n + 1)].bitcast(FP8X4),
+                    lhsT_scale=w3_sc[a][:, P * n : P * (n + 1)],
+                    rhs=x_codes[a][:, lo : lo + HALF].bitcast(FP8X4),
+                    rhs_scale=x_sc[a][:, lo : lo + HALF],
+                    start=(a == 0), stop=(a == 1),
+                )
+
+        def bound(h, n, scratch):
+            e = banks[e_banks[h][n]][:]
+            nc.scalar.activation(scratch[:, 0:HALF], e, ACT.Abs)
+            nc.scalar.activation(scratch[:, HALF:PK], scratch[:, 0:HALF], ACT.Abs_reciprocal_sqrt, bias=1.0)
+            nc.scalar.activation(inv(h, n), scratch[:, HALF:PK], ACT.Square)
+
+        def scaled(h, n, ew):
+            nc.vector.tensor_tensor(
+                ew[:, n, :], banks[e_banks[h][n]][:], wo[:, HALF * h : HALF * (h + 1)], ALU.mult
+            )
+
+        def place(h, n, ew):
+            nc.vector.tensor_tensor(
+                liners[n][:].indirect(cols(out_list, HALF * h, HALF * (h + 1))),
+                ew[:, n, :], inv(h, n), ALU.mult,
+            )
+
+        ew0 = sb("ew0", [P, 4, HALF], F32, tag="wide")
+        first_scratch = sb("first_scratch", [P, PK], F32, tag="x1b")
+        for n in range(4):
+            third_product(0, n)
+        bound(0, 0, first_scratch)
+        scaled(0, 0, ew0)
+        bound(0, 1, turned[1])
+        for n in range(1, 4):
+            scaled(0, n, ew0)
+        x_bf1b = sb("x_bf1b", [P, 4 * HALF], BF16, tag="x1b")
+        place(0, 0, ew0)
+        weigh(6, got6[:, HALF:PK], x_bf1b[:])
+        weigh(7, got7[:, HALF:PK], x_bf1b[:])
+        place(0, 1, ew0)
+        bound(0, 2, turned[2])
+        weigh(4, got45[:, 0, :], x_bf1b[:])
+        weigh(5, got45[:, 1, :], x_bf1b[:])
+        place(0, 2, ew0)
+        nc.vector.quantize_mx(x_codes[1][:, HALF:PK].bitcast(FP8X4), x_sc[1][:, HALF:PK], x_bf1b[:])
+        bound(0, 3, turned[0])
+        place(0, 3, ew0)
+
+        ew1 = sb("ew1", [P, 4, HALF], F32, tag="wide")
+        for n in range(4):
+            third_product(1, n)
+        for n in range(4):
+            bound(1, n, turned[(n + 1) % TURN_RING])
+            scaled(1, n, ew1)
+        for n in range(4):
+            place(1, n, ew1)
+            nc.sync.dma_start(out[P * n : P * (n + 1), :], liners[n][:])

@@ -54,29 +54,32 @@ def tile_list_socket_liner_page_kernel(
         nc.vector.memset(tab_plane[:].bitcast(I32), 0)
         nc.vector.memset(w2_plane[:].bitcast(I32), 0)
 
-        nc.sync.dma_start(scan_list[:], offs)
-        w2_raw = sb("w2_raw", [P, 2 * H], U8)
-        nc.sync.dma_start(w2_raw[:].bitcast(I32), w2_words[0].bitcast(I32))
+        for lst, src in ((scan_list, offs), (put_list, offs2), (recall_list, offs3), (out_list, offs4)):
+            nc.sync.dma_start(lst[:], src)
+        g1 = sb("g1", [P, 4], F32)
+        nc.sync.dma_start(g1[:], gain1.rearrange("(p t) -> p t", t=4))
+        g2 = [sb("g2_%d" % a, [P, 4], F32) for a in range(2)]
+        for a in range(2):
+            nc.sync.dma_start(g2[a][:], gain2.rearrange("(a p t) -> a p t", a=2, t=4)[a])
+        w1_raw = [sb("w1_raw%d" % a, [P, 4, M], F32, tag="w_raw%d" % a) for a in range(2)]
+        w1_rows = w1.rearrange("(a p j) m -> a p j m", a=2, j=4)
+        nc.sync.dma_start(w1_raw[0][:], w1_rows[0])
         for q in range(4):
-            nc.scalar.dma_start(
+            nc.sync.dma_start(
                 tab_plane[32 * q : 32 * q + 8, :].bitcast(I32),
                 tab_scales[:, 4 * q : 4 * q + 4, :].bitcast(I32),
             )
-        for q in range(4):
-            nc.scalar.dma_start(
-                w2_plane[32 * q : 32 * q + 4, :].bitcast(I32),
-                w2_scales[0, 4 * q : 4 * q + 4, :].bitcast(I32),
-            )
-        w1_raw = [sb("w1_raw%d" % a, [P, 4, M], F32, tag="w_raw%d" % a) for a in range(2)]
-        for a in range(2):
-            nc.sync.dma_start(
-                w1_raw[a][:], w1[HALF * a : HALF * (a + 1), :].rearrange("(p j) m -> p j m", j=4)
-            )
+        nc.sync.dma_start(w1_raw[1][:], w1_rows[1])
         tab = [sb("tab%d" % a, [P, T], I32, tag="tab%d" % a) for a in range(2)]
         for a in range(2):
             nc.sync.dma_start(tab[a][:], tab_words[a].rearrange("p t i -> p (t i)").bitcast(I32))
-        g1 = sb("g1", [P, 4], F32)
-        nc.sync.dma_start(g1[:], gain1.rearrange("(p t) -> p t", t=4))
+        w2_raw = sb("w2_raw", [P, H], U16)
+        nc.sync.dma_start(w2_raw[:].bitcast(I32), w2_words[0].bitcast(I32))
+        for q in range(4):
+            nc.sync.dma_start(
+                w2_plane[32 * q : 32 * q + 4, :].bitcast(I32),
+                w2_scales[0, 4 * q : 4 * q + 4, :].bitcast(I32),
+            )
 
         rest_rows = rest.rearrange("(a p t) j -> a t p j", a=2, t=4)
         page_rows = page0.rearrange("(a p t) c -> a t p c", a=2, t=4)
@@ -85,7 +88,6 @@ def tile_list_socket_liner_page_kernel(
         pages = [sb("page%d" % s, [P, T2], F32) for s in range(SLICES)]
         wg_first = sb("wg_first", [P, S], F32)
         wg_rest = sb("wg_rest", [P, 3, S], F32)
-        g2 = sb("g2", [P, 2, 4], F32)
 
         def rest_tile(s):
             return ring[s % REST_RING]
@@ -97,7 +99,6 @@ def tile_list_socket_liner_page_kernel(
         def load_slice(s):
             nc.sync.dma_start(rest_tile(s)[:], rest_rows[s // 4, s % 4])
             if s == 0:
-                nc.sync.dma_start(put_list[:], offs2)
                 for u in range(4):
                     nc.sync.dma_start(wg_first[32 * u : 32 * u + 32, :], wgs_rows[:, 0, :])
             nc.sync.dma_start(pages[s][:], page_rows[s // 4, s % 4])
@@ -108,25 +109,12 @@ def tile_list_socket_liner_page_kernel(
 
         load_slice(0)
         nc.sync.dma_start(pages[1][:], page_rows[0, 1])
-        nc.sync.dma_start(recall_list[:], offs3)
-        nc.sync.dma_start(g2[:], gain2.rearrange("(a p t) -> p a t", a=2, t=4))
         for s in range(2, REST_RING):
             load_slice(s)
 
         ident = sb("ident", [P, P], F32)
         make_identity(nc, ident[:])
 
-        w2_dealt = sb("w2_dealt", [P, SLICES, 2 * P], U8)
-        w2_sc = sb("w2_sc", [P, SLICES, P], U8)
-        for a in range(2):
-            nc.vector.tensor_copy(
-                w2_dealt[:, 4 * a : 4 * a + 4, :].rearrange("p t (q b) -> p t q b", b=2),
-                w2_raw[:, H * a : H * (a + 1)].rearrange("p (q t b) -> p t q b", t=4, b=2),
-            )
-        nc.vector.tensor_copy(
-            w2_sc[:].rearrange("p (a t) q -> p a t q", a=2),
-            w2_plane[:].rearrange("p (a q t) -> p a t q", a=2, t=4),
-        )
         v_sc = sb("v_sc", [P, S], U8)
         nc.vector.tensor_copy(v_sc[:], tab_plane[:].indirect(scan_list[:]))
 
@@ -139,19 +127,25 @@ def tile_list_socket_liner_page_kernel(
             if a == 0:
                 nc.scalar.copy(dst, src)
             else:
-                nc.vector.tensor_copy(dst, src)
+                nc.scalar.copy(dst[:, :, 0:2, :], src[:, :, 0:2, :])
+                nc.vector.tensor_copy(dst[:, :, 2:4, :], src[:, :, 2:4, :])
         for a in range(2):
             nc.vector.quantize_mx(w1_codes[a][:].bitcast(FP8X4), w1_sc[a][:], w1_bf[a][:])
 
         v_codes = [sb("v_codes%d" % a, [P, S], U32, tag="codes%d" % a) for a in range(2)]
-        for lo in range(0, S, HALF):
-            nc.vector.tensor_copy(
-                v_codes[0][:, lo : lo + HALF], tab[0][:].bitcast(U32).indirect(cols(scan_list, lo, lo + HALF))
-            )
         for lo in range(0, S, QUARTER):
+            for a in range(2):
+                nc.vector.tensor_copy(
+                    v_codes[a][:, lo : lo + QUARTER],
+                    tab[a][:].bitcast(U32).indirect(cols(scan_list, lo, lo + QUARTER)),
+                )
+
+        w2_dealt = sb("w2_dealt", [P, SLICES, P], U16)
+        w2_sc = sb("w2_sc", [P, SLICES, P], U8)
+        for dealt, raw in ((w2_dealt, w2_raw), (w2_sc, w2_plane)):
             nc.vector.tensor_copy(
-                v_codes[1][:, lo : lo + QUARTER],
-                tab[1][:].bitcast(U32).indirect(cols(scan_list, lo, lo + QUARTER)),
+                dealt[:].rearrange("p (a t) q -> p a t q", a=2),
+                raw[:].rearrange("p (a q t) -> p a t q", a=2, t=4),
             )
 
         th = sb("th", [P, 2, 4 * QUARTER], F32, tag="wide")
@@ -176,11 +170,16 @@ def tile_list_socket_liner_page_kernel(
 
         def features(q):
             lo, hi, i = QUARTER * q, QUARTER * (q + 1), q % 2
-            for t in range(4):
-                bank = banks[2 * i + t // 2]
-                for a in range(2):
+            if q < 2:
+                sums = [banks[4 * q + t][:, 0:QUARTER] for t in range(4)]
+                order = [(t, a) for a in range(2) for t in range(4)]
+            else:
+                sums = [banks[2 * i + t // 2][:, QUARTER * (t % 2) : QUARTER * (t % 2 + 1)] for t in range(4)]
+                order = [(t, a) for t in range(4) for a in range(2)]
+            for t, a in order:
+                if True:
                     nc.tensor.matmul_mx(
-                        bank[:, QUARTER * (t % 2) : QUARTER * (t % 2 + 1)],
+                        sums[t],
                         lhsT=w1_codes[a][:, P * t : P * (t + 1)].bitcast(FP8X4),
                         lhsT_scale=w1_sc[a][:, P * t : P * (t + 1)],
                         rhs=v_codes[a][:, lo:hi].bitcast(FP8X4),
@@ -188,13 +187,17 @@ def tile_list_socket_liner_page_kernel(
                         start=(a == 0), stop=(a == 1),
                     )
             for u in range(2):
-                nc.scalar.activation(th[:, i, HALF * u : HALF * (u + 1)], banks[2 * i + u][:], ACT.Tanh)
+                if q >= 2:
+                    nc.scalar.activation(th[:, i, HALF * u : HALF * (u + 1)], banks[2 * i + u][:], ACT.Tanh)
                 for t in (2 * u, 2 * u + 1):
+                    if q < 2:
+                        nc.scalar.activation(th[:, i, QUARTER * t : QUARTER * (t + 1)], sums[t], ACT.Tanh)
                     nc.scalar.activation(
                         f_planes[i][:, t, :], th[:, i, QUARTER * t : QUARTER * (t + 1)],
                         ACT.Copy, scale=g1[:, t : t + 1],
                     )
-            nc.vector.tensor_copy(
+            weave = nc.vector.tensor_copy if q < 2 else nc.scalar.copy
+            weave(
                 f_bf[i][:].rearrange("p (c k t) -> p c t k", k=4, t=4),
                 f_planes[i][:].rearrange("p t (c k) -> p c t k", k=4),
             )
@@ -202,7 +205,7 @@ def tile_list_socket_liner_page_kernel(
 
         def first_slice(q):
             lo, hi = QUARTER * q, QUARTER * (q + 1)
-            bank = banks[4 + q % 2]
+            bank = banks[(4, 2, 5, 4)[q]]
             second_product(0, lo, hi, bank)
             nc.vector.tensor_tensor(
                 rest_tile(0)[:, lo:hi], bank[:, 0:QUARTER], rest_tile(0)[:, lo:hi], ALU.subtract
@@ -210,9 +213,11 @@ def tile_list_socket_liner_page_kernel(
             put(0, lo, hi)
 
         features(0)
-        for q in range(4):
-            if q + 1 < 4:
-                features(q + 1)
+        features(1)
+        first_slice(0)
+        features(2)
+        features(3)
+        for q in range(1, 4):
             first_slice(q)
 
         neg = [sb("neg%d" % i, [P, S], F32) for i in range(NEG_RING)]
@@ -248,7 +253,7 @@ def tile_list_socket_liner_page_kernel(
         def weigh(s, src, dst):
             a, t = s // 4, s % 4
             nc.scalar.activation(
-                dst.rearrange("p (c t) -> p c t", t=4)[:, :, t], src, ACT.Copy, scale=g2[:, a, t : t + 1]
+                dst.rearrange("p (c t) -> p c t", t=4)[:, :, t], src, ACT.Copy, scale=g2[a][:, t : t + 1]
             )
 
         x_codes = [sb("x_codes%d" % a, [P, PK], U32, tag="codes%d" % a) for a in range(2)]
@@ -292,11 +297,13 @@ def tile_list_socket_liner_page_kernel(
             if s in (1, 2):
                 quantize_w3(s - 1)
             if s == 3:
+                warm = sb("warm", [P, 1], F32)
+                nc.scalar.activation(warm[:], rest_tile(6)[:, 0:1], ACT.Abs_reciprocal_sqrt, scale=0.0, bias=1.0)
+            if s == 3:
                 nc.vector.quantize_mx(x_codes[0][:].bitcast(FP8X4), x_sc[0][:], x_bf0[:])
 
         wo = sb("wo", [P, PK], F32)
         nc.sync.dma_start(wo[:], wgo)
-        nc.sync.dma_start(out_list[:], offs4)
         liner_tags = ("tab0", "tab1", "w_raw0", "w_raw1")
         liners = [sb("liner%d" % n, [P, T2], F32, tag=liner_tags[n]) for n in range(4)]
         for n in range(4):
@@ -357,14 +364,18 @@ def tile_list_socket_liner_page_kernel(
         bound(0, 1, turned[1])
         for n in range(1, 4):
             scaled(0, n, ew0)
-        x_bf1b = sb("x_bf1b", [P, 4 * HALF], BF16, tag="x1b")
+        x_planes = sb("x_planes", [P, 4, HALF], BF16, tag="x1b")
+        x_bf1b = sb("x_bf1b", [P, 4 * HALF], BF16, tag="w_bf0")
         place(0, 0, ew0)
-        weigh(6, got6[:, HALF:PK], x_bf1b[:])
-        weigh(7, got7[:, HALF:PK], x_bf1b[:])
+        late = (got45[:, 0, :], got45[:, 1, :], got6[:, HALF:PK], got7[:, HALF:PK])
+        for t in (2, 3, 0, 1):
+            nc.scalar.activation(x_planes[:, t, :], late[t], ACT.Copy, scale=g2[1][:, t : t + 1])
         place(0, 1, ew0)
         bound(0, 2, turned[2])
-        weigh(4, got45[:, 0, :], x_bf1b[:])
-        weigh(5, got45[:, 1, :], x_bf1b[:])
+        nc.scalar.copy(
+            x_bf1b[:].rearrange("p (c k t) -> p c t k", k=4, t=4),
+            x_planes[:].rearrange("p t (c k) -> p c t k", k=4),
+        )
         place(0, 2, ew0)
         nc.vector.quantize_mx(x_codes[1][:, HALF:PK].bitcast(FP8X4), x_sc[1][:, HALF:PK], x_bf1b[:])
         bound(0, 3, turned[0])

@@ -86,31 +86,32 @@ def tile_list_socket_liner_page_kernel(
         wgs_rows = wgs.rearrange("(q t) j -> q t j", t=4)
         ring = [sb("ring%d" % i, [P, S], F32) for i in range(REST_RING)]
         pages = [sb("page%d" % s, [P, T2], F32) for s in range(SLICES)]
-        wg_first = sb("wg_first", [P, S], F32)
-        wg_rest = sb("wg_rest", [P, 3, S], F32)
+        wg = [sb("wg%d" % t, [P, S], F32) for t in range(4)]
 
         def rest_tile(s):
             return ring[s % REST_RING]
 
-        def wg(s):
-            t = s % 4
-            return wg_first[:] if t == 0 else wg_rest[:, t - 1, :]
+        def load_wg(t, lo, hi):
+            for u in (0, 2, 1, 3):
+                nc.sync.dma_start(wg[t][32 * u : 32 * u + 32, lo:hi], wgs_rows[:, t, lo:hi])
 
-        def load_slice(s):
+        def load_rest(s):
             nc.sync.dma_start(rest_tile(s)[:], rest_rows[s // 4, s % 4])
-            if s == 0:
-                for u in range(4):
-                    nc.sync.dma_start(wg_first[32 * u : 32 * u + 32, :], wgs_rows[:, 0, :])
-            nc.sync.dma_start(pages[s][:], page_rows[s // 4, s % 4])
-            if s == 0:
-                nc.sync.dma_start(rest_tile(1)[:], rest_rows[0, 1])
-                for u in range(4):
-                    nc.sync.dma_start(wg_rest[32 * u : 32 * u + 32, :, :], wgs_rows[:, 1:4, :])
 
-        load_slice(0)
-        nc.sync.dma_start(pages[1][:], page_rows[0, 1])
-        for s in range(2, REST_RING):
-            load_slice(s)
+        def load_page(s):
+            nc.sync.dma_start(pages[s][:], page_rows[s // 4, s % 4])
+
+        load_rest(0)
+        load_page(0)
+        load_wg(0, 0, QUARTER)
+        load_rest(1)
+        load_wg(0, QUARTER, S)
+        for s in range(1, SLICES):
+            if s < 4:
+                load_wg(s, 0, S)
+            load_page(s)
+            if s + 1 < REST_RING:
+                load_rest(s + 1)
 
         ident = sb("ident", [P, P], F32)
         make_identity(nc, ident[:])
@@ -165,7 +166,7 @@ def tile_list_socket_liner_page_kernel(
         def put(s, lo, hi):
             nc.vector.tensor_tensor(
                 pages[s][:].indirect(cols(put_list, lo, hi)),
-                rest_tile(s)[:, lo:hi], wg(s)[:, lo:hi], ALU.mult,
+                rest_tile(s)[:, lo:hi], wg[s % 4][:, lo:hi], ALU.mult,
             )
 
         def features(q):
@@ -196,8 +197,8 @@ def tile_list_socket_liner_page_kernel(
                         f_planes[i][:, t, :], th[:, i, QUARTER * t : QUARTER * (t + 1)],
                         ACT.Copy, scale=g1[:, t : t + 1],
                     )
-            weave = nc.vector.tensor_copy if q < 2 else nc.scalar.copy
-            weave(
+            copy = nc.vector.tensor_copy if q < 2 else nc.scalar.copy
+            copy(
                 f_bf[i][:].rearrange("p (c k t) -> p c t k", k=4, t=4),
                 f_planes[i][:].rearrange("p t (c k) -> p c t k", k=4),
             )
@@ -261,7 +262,6 @@ def tile_list_socket_liner_page_kernel(
         w3_codes = [sb("w3_codes%d" % a, [P, N], U32, tag="w_codes%d" % a) for a in range(2)]
         w3_sc = [sb("w3_sc%d" % a, [P, N], U8, tag="w_sc%d" % a) for a in range(2)]
         w3_raw = [sb("w3_raw%d" % a, [P, 4, N], F32, tag="w_raw%d" % a) for a in range(2)]
-        w3_bf = [sb("w3_bf%d" % a, [P, 4 * N], BF16, tag="w_bf%d" % a) for a in range(2)]
 
         def load_w3(a):
             nc.sync.dma_start(
@@ -269,13 +269,19 @@ def tile_list_socket_liner_page_kernel(
             )
 
         def quantize_w3(a):
+            w3_bf = sb("w3_bf%d" % a, [P, 4 * N], BF16, tag="w_bf%d" % a)
             nc.scalar.copy(
-                w3_bf[a][:].rearrange("p (c k j) -> p c j k", k=4, j=4),
+                w3_bf[:].rearrange("p (c k j) -> p c j k", k=4, j=4),
                 w3_raw[a][:].rearrange("p j (c k) -> p c j k", k=4),
             )
-            nc.vector.quantize_mx(w3_codes[a][:].bitcast(FP8X4), w3_sc[a][:], w3_bf[a][:])
+            nc.vector.quantize_mx(w3_codes[a][:].bitcast(FP8X4), w3_sc[a][:], w3_bf[:])
 
-        x_bf0 = sb("x_bf0", [P, 4 * PK], BF16, tag="wide")
+        def weave(dst, planes):
+            nc.scalar.copy(
+                dst.rearrange("p (c k t) -> p c t k", k=4, t=4), planes.rearrange("p t (c k) -> p c t k", k=4)
+            )
+
+        x_planes0 = sb("x_planes0", [P, 4, PK], BF16, tag="wide")
         x_bf1a = sb("x_bf1a", [P, 4 * HALF], BF16, tag="x1a")
 
         states(1)
@@ -286,21 +292,33 @@ def tile_list_socket_liner_page_kernel(
             got = turned[(s + 2) % TURN_RING]
             wide = PK if s < 4 else HALF
             recall(s, 0, wide, got[:, 0:wide])
+            if s == 5:
+                recall(6, 0, HALF, got[:, HALF:PK])
             put(s + 2, 0, S)
             if s + REST_RING < SLICES:
-                load_slice(s + REST_RING)
+                load_rest(s + REST_RING)
             if s in (0, 1):
                 load_w3(s)
             if s + 3 < SLICES:
                 states(s + 3)
-            weigh(s, got[:, 0:wide], x_bf0[:] if s < 4 else x_bf1a[:])
-            if s in (1, 2):
-                quantize_w3(s - 1)
+            if s < 4:
+                nc.scalar.activation(x_planes0[:, s, :], got[:], ACT.Copy, scale=g2[0][:, s : s + 1])
+            else:
+                weigh(s, got[:, 0:HALF], x_bf1a[:])
             if s == 3:
                 warm = sb("warm", [P, 1], F32)
                 nc.scalar.activation(warm[:], rest_tile(6)[:, 0:1], ACT.Abs_reciprocal_sqrt, scale=0.0, bias=1.0)
+            if s in (1, 2):
+                quantize_w3(s - 1)
             if s == 3:
-                nc.vector.quantize_mx(x_codes[0][:].bitcast(FP8X4), x_sc[0][:], x_bf0[:])
+                for h in range(2):
+                    x_bf0 = sb("x_bf0_%d" % h, [P, 4 * HALF], BF16, tag="w_bf%d" % (1 - h))
+                    weave(x_bf0[:], x_planes0[:, :, HALF * h : HALF * (h + 1)])
+                    nc.vector.quantize_mx(
+                        x_codes[0][:, HALF * h : HALF * (h + 1)].bitcast(FP8X4),
+                        x_sc[0][:, HALF * h : HALF * (h + 1)], x_bf0[:],
+                    )
+        weigh(6, turned[7 % TURN_RING][:, HALF:PK], x_bf1a[:])
 
         wo = sb("wo", [P, PK], F32)
         nc.sync.dma_start(wo[:], wgo)
@@ -309,11 +327,10 @@ def tile_list_socket_liner_page_kernel(
         for n in range(4):
             nc.sync.dma_start(liners[n][:], page1[P * n : P * (n + 1), :])
 
-        got6, got7 = rest_tile(7), neg[7 % NEG_RING]
-        for lo in (0, HALF):
-            recall(6, lo, lo + HALF, got6[:, lo : lo + HALF])
-            recall(7, lo, lo + HALF, got7[:, lo : lo + HALF])
-        weigh(6, got6[:, 0:HALF], x_bf1a[:])
+        got6, got7 = rest_tile(7), neg[0]
+        recall(7, 0, HALF, got7[:, 0:HALF])
+        recall(6, HALF, PK, got6[:, HALF:PK])
+        recall(7, HALF, PK, got7[:, HALF:PK])
         weigh(7, got7[:, 0:HALF], x_bf1a[:])
         nc.vector.quantize_mx(x_codes[1][:, 0:HALF].bitcast(FP8X4), x_sc[1][:, 0:HALF], x_bf1a[:])
         got45 = sb("got45", [P, 2, HALF], F32, tag="x1a")
@@ -361,9 +378,9 @@ def tile_list_socket_liner_page_kernel(
             third_product(0, n)
         bound(0, 0, first_scratch)
         scaled(0, 0, ew0)
-        bound(0, 1, turned[1])
         for n in range(1, 4):
             scaled(0, n, ew0)
+        bound(0, 1, turned[1])
         x_planes = sb("x_planes", [P, 4, HALF], BF16, tag="x1b")
         x_bf1b = sb("x_bf1b", [P, 4 * HALF], BF16, tag="w_bf0")
         place(0, 0, ew0)
@@ -372,10 +389,7 @@ def tile_list_socket_liner_page_kernel(
             nc.scalar.activation(x_planes[:, t, :], late[t], ACT.Copy, scale=g2[1][:, t : t + 1])
         place(0, 1, ew0)
         bound(0, 2, turned[2])
-        nc.scalar.copy(
-            x_bf1b[:].rearrange("p (c k t) -> p c t k", k=4, t=4),
-            x_planes[:].rearrange("p t (c k) -> p c t k", k=4),
-        )
+        weave(x_bf1b[:], x_planes[:])
         place(0, 2, ew0)
         nc.vector.quantize_mx(x_codes[1][:, HALF:PK].bitcast(FP8X4), x_sc[1][:, HALF:PK], x_bf1b[:])
         bound(0, 3, turned[0])

from contextlib import ExitStack

import concourse.mybir as mybir
from concourse.masks import make_identity

K, T, S, M, H, N, T2, PK = 1024, 2048, 1024, 512, 1024, 512, 2048, 1024
FLOPS = 2 * K * M * S + 2 * M * H * S + 2 * H * N * PK

F32 = mybir.dt.float32
BF16 = mybir.dt.bfloat16
I32 = mybir.dt.int32
U32 = mybir.dt.uint32
U16 = mybir.dt.uint16
U8 = mybir.dt.uint8
FP8X4 = mybir.dt.float8_e4m3fn_x4
FP4X4 = mybir.dt.float4_e2m1fn_x4
ACT = mybir.ActivationFunctionType
ALU = mybir.AluOpType

P = 128
QUARTER = 256
HALF = 512
SLICES = 8
REST_RING = 5
NEG_RING = 2
TURN_RING = 3


def tile_list_socket_liner_page_kernel(
    tc, tab_words, tab_scales, offs, w1, gain1, w2_words, w2_scales, rest, wgs,
    page0, offs2, offs3, gain2, w3, wgo, page1, offs4, out,
):
    nc = tc.nc
    with ExitStack() as ctx:
        lists = ctx.enter_context(tc.tile_pool(name="lists", bufs=1))
        pool = ctx.enter_context(tc.tile_pool(name="pool", bufs=1))
        psum = ctx.enter_context(tc.psum_pool(name="psum", bufs=1))

        def sb(name, shape, dtype, tag=None):
            return pool.tile(shape, dtype, name=name, tag=tag or name, align_bytes=64)

        def cols(lst, lo, hi):
            return lst[:, lo // 16 : hi // 16]

        banks = [psum.tile([P, HALF], F32, name="bank%d" % b) for b in range(8)]

        scan_list = lists.tile([P, S // 16], U16, name="scan_list")
        put_list = lists.tile([P, S // 16], U16, name="put_list")
        recall_list = lists.tile([P, PK // 16], U16, name="recall_list")
        out_list = lists.tile([P, PK // 16], U16, name="out_list")

        tab_plane = sb("tab_plane", [P, T], U8)
        w2_plane = sb("w2_plane", [P, H], U8)
        nc.vector.memset(tab_plane[:].bitcast(I32), 0)
        nc.vector.memset(w2_plane[:].bitcast(I32), 0)

        for lst, src in ((scan_list, offs), (put_list, offs2), (recall_list, offs3), (out_list, offs4)):
            nc.sync.dma_start(lst[:], src)
        g1 = sb("g1", [P, 4], F32)
        nc.sync.dma_start(g1[:], gain1.rearrange("(p t) -> p t", t=4))
        g2 = [sb("g2_%d" % a, [P, 4], F32) for a in range(2)]
        for a in range(2):
            nc.sync.dma_start(g2[a][:], gain2.rearrange("(a p t) -> a p t", a=2, t=4)[a])
        w1_raw = [sb("w1_raw%d" % a, [P, 4, M], F32, tag="w_raw%d" % a) for a in range(2)]
        w1_rows = w1.rearrange("(a p j) m -> a p j m", a=2, j=4)
        nc.sync.dma_start(w1_raw[0][:], w1_rows[0])
        for q in range(4):
            nc.sync.dma_start(
                tab_plane[32 * q : 32 * q + 8, :].bitcast(I32),
                tab_scales[:, 4 * q : 4 * q + 4, :].bitcast(I32),
            )
        nc.sync.dma_start(w1_raw[1][:], w1_rows[1])
        tab = [sb("tab%d" % a, [P, T], I32, tag="tab%d" % a) for a in range(2)]
        for a in range(2):
            nc.sync.dma_start(tab[a][:], tab_words[a].rearrange("p t i -> p (t i)").bitcast(I32))
        w2_raw = sb("w2_raw", [P, H], U16)
        nc.sync.dma_start(w2_raw[:].bitcast(I32), w2_words[0].bitcast(I32))
        for q in range(4):
            nc.sync.dma_start(
                w2_plane[32 * q : 32 * q + 4, :].bitcast(I32),
                w2_scales[0, 4 * q : 4 * q + 4, :].bitcast(I32),
            )

        rest_rows = rest.rearrange("(a p t) j -> a t p j", a=2, t=4)
        page_rows = page0.rearrange("(a p t) c -> a t p c", a=2, t=4)
        wgs_rows = wgs.rearrange("(q t) j -> q t j", t=4)
        ring = [sb("ring%d" % i, [P, S], F32) for i in range(REST_RING)]
        pages = [sb("page%d" % s, [P, T2], F32) for s in range(SLICES)]
        wg = [sb("wg%d" % t, [P, S], F32) for t in range(4)]

        def rest_tile(s):
            return ring[s % REST_RING]

        def load_wg(t, lo, hi):
            for u in (0, 2, 1, 3):
                nc.sync.dma_start(wg[t][32 * u : 32 * u + 32, lo:hi], wgs_rows[:, t, lo:hi])

        def load_rest(s):
            nc.sync.dma_start(rest_tile(s)[:], rest_rows[s // 4, s % 4])

        def load_page(s):
            nc.sync.dma_start(pages[s][:], page_rows[s // 4, s % 4])

        load_rest(0)
        load_page(0)
        load_wg(0, 0, QUARTER)
        load_rest(1)
        load_wg(0, QUARTER, S)
        for s in range(1, SLICES):
            if s < 4:
                load_wg(s, 0, S)
            load_page(s)
            if s + 1 < REST_RING:
                load_rest(s + 1)

        ident = sb("ident", [P, P], F32)
        make_identity(nc, ident[:])

        v_sc = sb("v_sc", [P, S], U8)
        nc.vector.tensor_copy(v_sc[:], tab_plane[:].indirect(scan_list[:]))

        w1_bf = [sb("w1_bf%d" % a, [P, 4 * M], BF16, tag="w_bf%d" % a) for a in range(2)]
        w1_codes = [sb("w1_codes%d" % a, [P, M], U32, tag="w_codes%d" % a) for a in range(2)]
        w1_sc = [sb("w1_sc%d" % a, [P, M], U8, tag="w_sc%d" % a) for a in range(2)]
        for a in range(2):
            dst = w1_bf[a][:].rearrange("p (t m j) -> p m t j", t=4, j=4)
            src = w1_raw[a][:].rearrange("p j (m t) -> p m t j", t=4)
            if a == 0:
                nc.scalar.copy(dst, src)
            else:
                nc.scalar.copy(dst[:, :, 0:2, :], src[:, :, 0:2, :])
                nc.vector.tensor_copy(dst[:, :, 2:4, :], src[:, :, 2:4, :])
        for a in range(2):
            nc.vector.quantize_mx(w1_codes[a][:].bitcast(FP8X4), w1_sc[a][:], w1_bf[a][:])

        v_codes = [sb("v_codes%d" % a, [P, S], U32, tag="codes%d" % a) for a in range(2)]
        for lo in range(0, S, QUARTER):
            for a in range(2):
                nc.vector.tensor_copy(
                    v_codes[a][:, lo : lo + QUARTER],
                    tab[a][:].bitcast(U32).indirect(cols(scan_list, lo, lo + QUARTER)),
                )

        w2_dealt = sb("w2_dealt", [P, SLICES, P], U16)
        w2_sc = sb("w2_sc", [P, SLICES, P], U8)
        for dealt, raw in ((w2_dealt, w2_raw), (w2_sc, w2_plane)):
            nc.vector.tensor_copy(
                dealt[:].rearrange("p (a t) q -> p a t q", a=2),
                raw[:].rearrange("p (a q t) -> p a t q", a=2, t=4),
            )

        th = sb("th", [P, 2, 4 * QUARTER], F32, tag="wide")
        f_planes = [sb("f_planes%d" % i, [P, 4, QUARTER], BF16) for i in range(2)]
        f_bf = [sb("f_bf%d" % i, [P, 4 * QUARTER], BF16) for i in range(2)]
        f_codes = sb("f_codes", [P, S], U32)
        f_sc = sb("f_sc", [P, S], U8)

        def second_product(s, lo, hi, bank):
            nc.tensor.matmul_mx(
                bank[:, 0 : hi - lo],
                lhsT=w2_dealt[:, s, :].bitcast(FP4X4), lhsT_scale=w2_sc[:, s, :],
                rhs=f_codes[:, lo:hi].bitcast(FP8X4), rhs_scale=f_sc[:, lo:hi],
                start=True, stop=True,
            )

        def put(s, lo, hi):
            nc.vector.tensor_tensor(
                pages[s][:].indirect(cols(put_list, lo, hi)),
                rest_tile(s)[:, lo:hi], wg[s % 4][:, lo:hi], ALU.mult,
            )

        def features(q):
            lo, hi, i = QUARTER * q, QUARTER * (q + 1), q % 2
            if q < 2:
                sums = [banks[4 * q + t][:, 0:QUARTER] for t in range(4)]
                order = [(t, a) for a in range(2) for t in range(4)]
            else:
                sums = [banks[2 * i + t // 2][:, QUARTER * (t % 2) : QUARTER * (t % 2 + 1)] for t in range(4)]
                order = [(t, a) for t in range(4) for a in range(2)]
            for t, a in order:
                if True:
                    nc.tensor.matmul_mx(
                        sums[t],
                        lhsT=w1_codes[a][:, P * t : P * (t + 1)].bitcast(FP8X4),
                        lhsT_scale=w1_sc[a][:, P * t : P * (t + 1)],
                        rhs=v_codes[a][:, lo:hi].bitcast(FP8X4),
                        rhs_scale=v_sc[4 * a : P, lo:hi],
                        start=(a == 0), stop=(a == 1),
                    )
            for u in range(2):
                if q >= 2:
                    nc.scalar.activation(th[:, i, HALF * u : HALF * (u + 1)], banks[2 * i + u][:], ACT.Tanh)
                for t in (2 * u, 2 * u + 1):
                    if q < 2:
                        nc.scalar.activation(th[:, i, QUARTER * t : QUARTER * (t + 1)], sums[t], ACT.Tanh)
                    nc.scalar.activation(
                        f_planes[i][:, t, :], th[:, i, QUARTER * t : QUARTER * (t + 1)],
                        ACT.Copy, scale=g1[:, t : t + 1],
                    )
            copy = nc.vector.tensor_copy if q < 2 else nc.scalar.copy
            copy(
                f_bf[i][:].rearrange("p (c k t) -> p c t k", k=4, t=4),
                f_planes[i][:].rearrange("p t (c k) -> p c t k", k=4),
            )
            nc.vector.quantize_mx(f_codes[:, lo:hi].bitcast(FP8X4), f_sc[:, lo:hi], f_bf[i][:])

        def first_slice(q):
            lo, hi = QUARTER * q, QUARTER * (q + 1)
            bank = banks[(4, 2, 5, 4)[q]]
            second_product(0, lo, hi, bank)
            nc.vector.tensor_tensor(
                rest_tile(0)[:, lo:hi], bank[:, 0:QUARTER], rest_tile(0)[:, lo:hi], ALU.subtract
            )
            put(0, lo, hi)

        features(0)
        features(1)
        first_slice(0)
        features(2)
        features(3)
        for q in range(1, 4):
            first_slice(q)

        neg = [sb("neg%d" % i, [P, S], F32) for i in range(NEG_RING)]
        turned = [sb("turned%d" % i, [P, S], F32) for i in range(TURN_RING)]

        def states(s):
            a_t, b_t, r_t = neg[s % NEG_RING], turned[s % TURN_RING], rest_tile(s)
            for h in range(2):
                lo = HALF * h
                second_product(s, lo, lo + HALF, banks[4 + h])
                nc.scalar.activation(a_t[:, lo : lo + HALF], banks[4 + h][:], ACT.Copy, scale=-1.0)
            for h in range(2):
                lo = HALF * h
                for n, src in enumerate((r_t, a_t)):
                    for c in range(4):
                        nc.tensor.matmul(
                            banks[6 + h][:, P * c : P * (c + 1)],
                            lhsT=src[:, lo + P * c : lo + P * (c + 1)], rhs=ident[:],
                            is_transpose=True, start=(n == 0 and c == 0), stop=(n == 1 and c == 3),
                        )
                nc.scalar.activation(b_t[:, lo : lo + HALF], banks[6 + h][:], ACT.Copy, scale=-1.0)
            for h in range(2):
                lo = HALF * h
                for c in range(4):
                    nc.tensor.transpose(
                        banks[h][:, P * c : P * (c + 1)], b_t[:, lo + P * c : lo + P * (c + 1)], ident[:]
                    )
                nc.scalar.copy(r_t[:, lo : lo + HALF], banks[h][:])

        def recall(s, lo, hi, dst):
            nc.vector.tensor_copy(dst, pages[s][:].indirect(cols(recall_list, lo, hi)))

        def weigh(s, src, dst):
            a, t = s // 4, s % 4
            nc.scalar.activation(
                dst.rearrange("p (c t) -> p c t", t=4)[:, :, t], src, ACT.Copy, scale=g2[a][:, t : t + 1]
            )

        x_codes = [sb("x_codes%d" % a, [P, PK], U32, tag="codes%d" % a) for a in range(2)]
        x_sc = [sb("x_sc%d" % a, [P, PK], U8) for a in range(2)]
        w3_codes = [sb("w3_codes%d" % a, [P, N], U32, tag="w_codes%d" % a) for a in range(2)]
        w3_sc = [sb("w3_sc%d" % a, [P, N], U8, tag="w_sc%d" % a) for a in range(2)]
        w3_raw = [sb("w3_raw%d" % a, [P, 4, N], F32, tag="w_raw%d" % a) for a in range(2)]

        def load_w3(a):
            nc.sync.dma_start(
                w3_raw[a][:], w3[HALF * a : HALF * (a + 1), :].rearrange("(p j) n -> p j n", j=4)
            )

        def quantize_w3(a):
            w3_bf = sb("w3_bf%d" % a, [P, 4 * N], BF16, tag="w_bf%d" % a)
            nc.scalar.copy(
                w3_bf[:].rearrange("p (c k j) -> p c j k", k=4, j=4),
                w3_raw[a][:].rearrange("p j (c k) -> p c j k", k=4),
            )
            nc.vector.quantize_mx(w3_codes[a][:].bitcast(FP8X4), w3_sc[a][:], w3_bf[:])

        def weave(dst, planes):
            nc.scalar.copy(
                dst.rearrange("p (c k t) -> p c t k", k=4, t=4), planes.rearrange("p t (c k) -> p c t k", k=4)
            )

        x_planes0 = sb("x_planes0", [P, 4, PK], BF16, tag="wide")
        x_bf1a = sb("x_bf1a", [P, 4 * HALF], BF16, tag="x1a")

        states(1)
        put(1, 0, HALF)
        put(1, HALF, S)
        states(2)
        for s in range(6):
            got = turned[(s + 2) % TURN_RING]
            wide = PK if s < 4 else HALF
            recall(s, 0, wide, got[:, 0:wide])
            if s == 5:
                recall(6, 0, HALF, got[:, HALF:PK])
            put(s + 2, 0, S)
            if s + REST_RING < SLICES:
                load_rest(s + REST_RING)
            if s in (0, 1):
                load_w3(s)
            if s + 3 < SLICES:
                states(s + 3)
            if s < 4:
                nc.scalar.activation(x_planes0[:, s, :], got[:], ACT.Copy, scale=g2[0][:, s : s + 1])
            else:
                weigh(s, got[:, 0:HALF], x_bf1a[:])
            if s == 3:
                warm = sb("warm", [P, 1], F32)
                nc.scalar.activation(warm[:], rest_tile(6)[:, 0:1], ACT.Abs_reciprocal_sqrt, scale=0.0, bias=1.0)
            if s in (1, 2):
                quantize_w3(s - 1)
            if s == 3:
                for h in range(2):
                    x_bf0 = sb("x_bf0_%d" % h, [P, 4 * HALF], BF16, tag="w_bf%d" % (1 - h))
                    weave(x_bf0[:], x_planes0[:, :, HALF * h : HALF * (h + 1)])
                    nc.vector.quantize_mx(
                        x_codes[0][:, HALF * h : HALF * (h + 1)].bitcast(FP8X4),
                        x_sc[0][:, HALF * h : HALF * (h + 1)], x_bf0[:],
                    )
        weigh(6, turned[7 % TURN_RING][:, HALF:PK], x_bf1a[:])

        wo = sb("wo", [P, PK], F32)
        nc.sync.dma_start(wo[:], wgo)
        liner_tags = ("tab0", "tab1", "w_raw0", "w_raw1")
        liners = [sb("liner%d" % n, [P, T2], F32, tag=liner_tags[n]) for n in range(4)]
        for n in range(4):
            nc.sync.dma_start(liners[n][:], page1[P * n : P * (n + 1), :])

        got6, got7 = rest_tile(7), neg[0]
        recall(7, 0, HALF, got7[:, 0:HALF])
        recall(6, HALF, PK, got6[:, HALF:PK])
        recall(7, HALF, PK, got7[:, HALF:PK])
        weigh(7, got7[:, 0:HALF], x_bf1a[:])
        nc.vector.quantize_mx(x_codes[1][:, 0:HALF].bitcast(FP8X4), x_sc[1][:, 0:HALF], x_bf1a[:])
        got45 = sb("got45", [P, 2, HALF], F32, tag="x1a")
        for i in range(2):
            recall(4 + i, HALF, PK, got45[:, i, :])

        e_banks = ((0, 1, 6, 7), (2, 3, 4, 5))
        inv_tiles = [ring[i] for i in (3, 4, 0, 1)]

        def inv(h, n):
            return inv_tiles[2 * h + n // 2][:, HALF * (n % 2) : HALF * (n % 2 + 1)]

        def third_product(h, n):
            lo = HALF * h
            for a in range(2):
                nc.tensor.matmul_mx(
                    banks[e_banks[h][n]][:],
                    lhsT=w3_codes[a][:, P * n : P * (n + 1)].bitcast(FP8X4),
                    lhsT_scale=w3_sc[a][:, P * n : P * (n + 1)],
                    rhs=x_codes[a][:, lo : lo + HALF].bitcast(FP8X4),
                    rhs_scale=x_sc[a][:, lo : lo + HALF],
                    start=(a == 0), stop=(a == 1),
                )

        def bound(h, n, scratch):
            e = banks[e_banks[h][n]][:]
            nc.scalar.activation(scratch[:, 0:HALF], e, ACT.Abs)
            nc.scalar.activation(scratch[:, HALF:PK], scratch[:, 0:HALF], ACT.Abs_reciprocal_sqrt, bias=1.0)
            nc.scalar.activation(inv(h, n), scratch[:, HALF:PK], ACT.Square)

        def scaled(h, n, ew):
            nc.vector.tensor_tensor(
                ew[:, n, :], banks[e_banks[h][n]][:], wo[:, HALF * h : HALF * (h + 1)], ALU.mult
            )

        def place(h, n, ew):
            nc.vector.tensor_tensor(
                liners[n][:].indirect(cols(out_list, HALF * h, HALF * (h + 1))),
                ew[:, n, :], inv(h, n), ALU.mult,
            )

        ew0 = sb("ew0", [P, 4, HALF], F32, tag="wide")
        first_scratch = sb("first_scratch", [P, PK], F32, tag="x1b")
        for n in range(4):
            third_product(0, n)
        bound(0, 0, first_scratch)
        scaled(0, 0, ew0)
        for n in range(1, 4):
            scaled(0, n, ew0)
        bound(0, 1, turned[1])
        x_planes = sb("x_planes", [P, 4, HALF], BF16, tag="x1b")
        x_bf1b = sb("x_bf1b", [P, 4 * HALF], BF16, tag="w_bf0")
        place(0, 0, ew0)
        late = (got45[:, 0, :], got45[:, 1, :], got6[:, HALF:PK], got7[:, HALF:PK])
        for t in (2, 3, 0, 1):
            nc.scalar.activation(x_planes[:, t, :], late[t], ACT.Copy, scale=g2[1][:, t : t + 1])
        place(0, 1, ew0)
        bound(0, 2, turned[2])
        weave(x_bf1b[:], x_planes[:])
        place(0, 2, ew0)
        nc.vector.quantize_mx(x_codes[1][:, HALF:PK].bitcast(FP8X4), x_sc[1][:, HALF:PK], x_bf1b[:])
        bound(0, 3, turned[0])
        place(0, 3, ew0)

        ew1 = sb("ew1", [P, 4, HALF], F32, tag="wide")
        for n in range(4):
            third_product(1, n)
        for n in range(4):
            bound(1, n, turned[(n + 1) % TURN_RING])
            scaled(1, n, ew1)
        for n in range(4):
            place(1, n, ew1)
            nc.sync.dma_start(out[P * n : P * (n + 1), :], liners[n][:])
